import numpy as np
import ml_dtypes

BF16 = ml_dtypes.bfloat16


def bf(x):
    return np.asarray(x, np.float32).astype(BF16)


def f32(x):
    return np.asarray(x, np.float32)


def f64(x):
    return np.asarray(x).astype(np.float64)


def striped(idx):
    return np.tile(idx.reshape(-1, 16).T, (8, 1))


S, K, M, N, D, V = 2048, 128, 512, 512, 16, 32


def setup_inputs():
    return {"table": bf(np.random.standard_normal((S, K))), "w": bf(np.random.standard_normal((K, M)) / np.sqrt(K)), "b": f32(0.5 * np.random.standard_normal((M, 1))), "offs": striped(np.random.permutation(S)[:N])}


def reference(table, w, b, offs):
    idx = offs[:16].T.reshape(-1)
    x = f64(table)[idx].T
    y = f64(w).T @ x
    z = np.tanh(y + f64(b))
    return z.reshape(M, V, D).max(axis=2)

import concourse.mybir as mybir
from concourse.masks import make_identity

S, K, M, N = 2048, 128, 512, 512
NEIGHBOURS = 16
POOLED = N // NEIGHBOURS
P = 128
CHUNK = 512
BLOCKS = CHUNK // P
FLOPS = 2 * K * M * N

BF16, F32, U16 = mybir.dt.bfloat16, mybir.dt.float32, mybir.dt.uint16
TANH = mybir.ActivationFunctionType.Tanh


def tile_gather_matmul_kernel(tc, table, w, b, offs, out):
    nc = tc.nc
    with (
        tc.tile_pool(name="held", bufs=1) as held,
        tc.tile_pool(name="rows", bufs=S // CHUNK) as rows_pool,
        tc.tile_pool(name="pooled", bufs=M // P) as pooled_pool,
        tc.psum_pool(name="flipped", bufs=4) as flip_pool,
        tc.psum_pool(name="products", bufs=4) as product_pool,
    ):
        row_tiles = []
        for c in range(S // CHUNK):
            rows = rows_pool.tile([P, BLOCKS, K], BF16, name="rows")
            queue = nc.sync if c % 2 == 0 else nc.scalar
            queue.dma_start(rows[:], table[c * CHUNK:(c + 1) * CHUNK, :].rearrange("(t p) k -> p t k", p=P))
            row_tiles.append(rows)
        offsets = held.tile([P, N // 16], U16, name="offsets")
        nc.sync.dma_start(offsets[:], offs)
        weights = held.tile([K, M], BF16, name="weights")
        nc.scalar.dma_start(weights[:], w)
        bias = held.tile([P, M // P], F32, name="bias")
        nc.scalar.dma_start(bias[:], b.rearrange("(a p) o -> p (a o)", p=P))

        warm = held.tile([P, 1], F32, name="warm")
        nc.vector.memset(warm[:], 0.0)
        nc.scalar.activation(warm[:], warm[:], TANH)

        identity = held.tile([P, P], BF16, name="identity")
        make_identity(nc, identity[:])

        window = held.tile([K, S], BF16, name="window")
        for c, rows in enumerate(row_tiles):
            flipped = flip_pool.tile([K, CHUNK], BF16, name="flipped")
            for t in range(BLOCKS):
                nc.tensor.transpose(flipped[:, t * P:(t + 1) * P], rows[:, t, :], identity[:])
            columns = window[:, c * CHUNK:(c + 1) * CHUNK]
            if c % 2 == 0:
                nc.vector.tensor_copy(columns, flipped[:])
            else:
                nc.scalar.copy(columns, flipped[:])

        for a in range(M // P):
            product = product_pool.tile([P, N], F32, name="product")
            nc.tensor.matmul(
                product[:], weights[:, a * P:(a + 1) * P], window[:].indirect(offsets[:]), start=True, stop=True
            )
            largest = pooled_pool.tile([P, POOLED], F32, name="largest")
            nc.vector.reduce_max(
                largest[:], product[:].rearrange("p (v t) -> p v t", t=NEIGHBOURS), axis=mybir.AxisListType.X
            )
            result = pooled_pool.tile([P, POOLED], F32, name="result")
            nc.scalar.activation(result[:], largest[:], TANH, bias=bias[:, a:a + 1])
            nc.sync.dma_start(out[a * P:(a + 1) * P, :], result[:])
